import numpy as np
import ml_dtypes


def mxq(x, axis, fmt="e4m3"):
    dtype, down = {"e4m3": (ml_dtypes.float8_e4m3fn, 7), "e5m2": (ml_dtypes.float8_e5m2, 14)}[fmt]
    v = np.moveaxis(np.asarray(x, np.float32).astype(ml_dtypes.bfloat16).astype(np.float64), axis, -1)
    blocks = v.reshape(v.shape[:-1] + (-1, 32))
    amax = np.abs(blocks).max(-1, keepdims=True)
    byte = np.maximum(np.where(amax > 0, np.frexp(amax)[1] - 1 + 127, 0) - down, 1)
    scale = np.exp2(byte - 127.0)
    codes = (blocks / scale).astype(np.float32).astype(dtype).astype(np.float64)
    return np.moveaxis((codes * scale).reshape(v.shape), -1, axis)


WIDE = False


def mx_kscale(k):
    if not WIDE:
        return np.ones(k)
    levels = np.array([10, -10, 5, -5, 0])
    if k % 512:
        return np.exp2(np.random.permutation(np.resize(levels, k // 32))).repeat(32)
    a = np.empty((k // 512, 16))
    for p in range(k // 512):
        a[p, :8] = np.random.permutation(np.resize(levels, 8))
        for g in range(8):
            far = levels[np.abs(levels - a[p, g]) >= 10]
            a[p, g + 8] = far[np.random.randint(len(far))]
    return np.exp2(a.ravel()).repeat(32)


def f64(x):
    return np.asarray(x).astype(np.float64)


def striped(idx):
    return np.tile(np.asarray(idx).reshape(-1, 16).T, (8, 1)).astype(np.uint16)


def unstriped(offs):
    return offs[:16].T.reshape(-1).astype(np.int64)


E2M1 = np.array([0.0, 0.5, 1.0, 1.5, 2.0, 3.0, 4.0, 6.0, -0.0, -0.5, -1.0, -1.5, -2.0, -3.0, -4.0, -6.0])


def pack_weight(w, fmt):
    k, n = w.shape
    w = f64(np.asarray(w, np.float32).astype(ml_dtypes.bfloat16)).reshape(k // 32, 32, n)
    amax = np.abs(w).max(1)
    if fmt == "e4m3":
        byte = np.frexp(amax)[1] - 1 + 127 - 7
    else:
        mant, ex = np.frexp(amax / 6.0)
        byte = np.where(mant > 0.5, ex, ex - 1) + 127
    byte = np.clip(np.where(amax > 0, byte, 1), 1, 254)
    scaled = (w * np.exp2(127.0 - byte)[:, None, :]).reshape(k, n).astype(np.float32)
    by_word = np.ascontiguousarray(scaled.reshape(k // 512, 128, 4, n).transpose(0, 1, 3, 2))
    if fmt == "e4m3":
        words = by_word.astype(ml_dtypes.float8_e4m3fn).view(np.uint8)
    else:
        c = by_word.astype(ml_dtypes.float4_e2m1fn).view(np.uint8) & 0xF
        words = (c[..., 0::2] | (c[..., 1::2] << 4)).reshape(k // 512, 128, 2 * n)
    return np.ascontiguousarray(words), np.ascontiguousarray(byte.astype(np.uint8).reshape(k // 512, 16, n))


def unpack_weight(words, scales, fmt):
    g, _, n = scales.shape
    words = np.ascontiguousarray(words).reshape(g, 128, n, -1)
    if fmt == "e4m3":
        vals = words.view(ml_dtypes.float8_e4m3fn).astype(np.float64)
    else:
        nib = np.empty((g, 128, n, 4), np.uint8)
        nib[..., 0::2] = words & 0xF
        nib[..., 1::2] = words >> 4
        vals = E2M1[nib]
    vals = vals * np.repeat(np.exp2(scales.astype(np.float64) - 127.0), 8, axis=1)[..., None]
    return vals.transpose(0, 1, 3, 2).reshape(g * 512, n)


K, L, T, S, J, N = 512, 512, 512, 512, 512, 512


def setup_inputs():
    n = np.random.standard_normal
    idx = np.random.randint(0, T, J)
    idx2 = np.random.randint(0, S, J)
    fk = mx_kscale(K)
    fl = mx_kscale(L)
    xap = pack_weight(n((K, T)) / fk[:, None], "e2m1")
    wap = pack_weight(n((K, N)) * 1 / np.sqrt(K) * fk[:, None], "e4m3")
    wbp = pack_weight(n((L, N)) * 1 / np.sqrt(L) * fl[:, None], "e2m1")
    return {
        "xa_words": xap[0],
        "xa_scales": xap[1],
        "wa_words": wap[0],
        "wa_scales": wap[1],
        "xb": (n((L, S)) / fl[:, None]).astype(np.float32),
        "wb_words": wbp[0],
        "wb_scales": wbp[1],
        "offs": striped(idx),
        "offs2": striped(idx2),
    }


def reference(xa_words, xa_scales, wa_words, wa_scales, xb, wb_words, wb_scales, offs, offs2):
    idx = unstriped(offs)
    idx2 = unstriped(offs2)
    xau = unpack_weight(xa_words, xa_scales, "e2m1")
    wau = unpack_weight(wa_words, wa_scales, "e4m3")
    wbu = unpack_weight(wb_words, wb_scales, "e2m1")
    za = wau.T @ xau
    xbq = mxq(f64(xb), 0, "e4m3")
    zb = wbu.T @ xbq
    u = za[:, idx] * zb[:, idx2]
    y = u / (1.0 + np.abs(za[:, idx]) + np.abs(zb[:, idx2]))
    return y

@@ -1,0 +1,209 @@
+from contextlib import ExitStack
+
+import concourse.mybir as mybir
+from concourse.masks import make_identity
+
+K = L = T = S = J = N = 512
+FLOPS = 2 * K * N * T + 2 * L * N * S
+
+F32 = mybir.dt.float32
+BF16 = mybir.dt.bfloat16
+I32 = mybir.dt.int32
+U32 = mybir.dt.uint32
+U16 = mybir.dt.uint16
+U8 = mybir.dt.uint8
+FP8X4 = mybir.dt.float8_e4m3fn_x4
+FP4X4 = mybir.dt.float4_e2m1fn_x4
+ALU = mybir.AluOpType
+ACT = mybir.ActivationFunctionType
+
+P = 128
+PACK = 4
+TILES = N // P
+SPARE = 192
+HALF = S // 2
+
+
+def load_scales(queue, plane, scales):
+    rows = scales[0].bitcast(I32)
+    for q in range(4):
+        four = rows[4 * q : 4 * q + 4, :]
+        queue.dma_start(
+            out=plane[32 * q : 32 * q + 32, :].bitcast(I32),
+            in_=four.unsqueeze(0).broadcast_to([8, 4, rows.shape[1]]),
+        )
+
+
+def tile_list_cross_lookup_product_kernel(
+    tc, xa_words, xa_scales, wa_words, wa_scales, xb, wb_words, wb_scales, offs, offs2, out
+):
+    nc = tc.nc
+    with ExitStack() as ctx:
+        keep = ctx.enter_context(tc.tile_pool(name="keep", bufs=1))
+        psum = ctx.enter_context(tc.psum_pool(name="psum", bufs=1))
+
+        xa_c = keep.tile([P, 2 * T], U8, name="xa_c", align_bytes=64)
+        xa_s = keep.tile([P, T], U8, name="xa_s", align_bytes=64)
+        wa_c = keep.tile([P, 4 * N], U8, name="wa_c", align_bytes=64)
+        wa_s = keep.tile([P, N], U8, name="wa_s", align_bytes=64)
+        wb_c = keep.tile([P, 2 * N], U8, name="wb_c", tag="wb_c", align_bytes=64)
+        wb_s = keep.tile([P, N], U8, name="wb_s", align_bytes=64)
+        list_a = keep.tile([P, J // 16], U16, name="list_a")
+        list_b = keep.tile([P, J // 16], U16, name="list_b")
+        xb_rows = xb.rearrange("(p j) w -> p j w", j=PACK)
+        xb_raw = [keep.tile([P, PACK, HALF], F32, name=f"xb_raw{h}", tag=f"xb_raw{h}") for h in range(2)]
+
+        load_scales(nc.sync, xa_s, xa_scales)
+        nc.sync.dma_start(out=xb_raw[0][:], in_=xb_rows[:, :, :HALF])
+        nc.sync.dma_start(out=xa_c[:].bitcast(I32), in_=xa_words[0].bitcast(I32))
+        nc.sync.dma_start(out=wa_c[:].bitcast(I32), in_=wa_words[0].rearrange("p n t -> p (n t)").bitcast(I32))
+        load_scales(nc.sync, wa_s, wa_scales)
+        nc.sync.dma_start(out=xb_raw[1][:], in_=xb_rows[:, :, HALF:])
+        nc.sync.dma_start(list_a[:], offs)
+        nc.sync.dma_start(out=wb_c[:].bitcast(I32), in_=wb_words[0].bitcast(I32))
+        load_scales(nc.sync, wb_s, wb_scales)
+        nc.sync.dma_start(list_b[:], offs2)
+
+        one = keep.tile([P, 1], F32, name="one")
+        warm = keep.tile([P, 1], F32, name="warm")
+        nc.vector.memset(one[:], 1.0)
+        nc.scalar.activation(out=warm[:], in_=one[:], func=ACT.Abs_reciprocal_sqrt)
+
+        za = keep.tile([P, TILES, T + SPARE], F32, name="za")
+        zb = [keep.tile([P, S + SPARE], F32, name=f"zb{i}", tag=f"zb{i}") for i in range(TILES)]
+        nc.vector.memset(za[:, :, T:], 0.0)
+        for i in range(TILES):
+            nc.gpsimd.memset(zb[i][:, S:], 0.0)
+        ident = keep.tile([P, P], F32, name="ident")
+        make_identity(nc, ident[:])
+
+        for i in range(TILES):
+            acc = psum.tile([P, T], F32, name=f"acc_a{i}", tag=f"pa{i}")
+            nc.tensor.matmul_mx(
+                out=acc[:],
+                lhsT=wa_c[:, 4 * P * i : 4 * P * (i + 1)].bitcast(FP8X4),
+                lhsT_scale=wa_s[:, P * i : P * (i + 1)],
+                rhs=xa_c[:].bitcast(FP4X4),
+                rhs_scale=xa_s[:],
+                start=True,
+                stop=True,
+            )
+            nc.scalar.copy(out=za[:, i, :T], in_=acc[:])
+
+        xb_c = keep.tile([P, S], U32, name="xb_c", tag="xb_c", align_bytes=64)
+        xb_s = keep.tile([P, S], U8, name="xb_s", align_bytes=64)
+        woven = keep.tile([P, S * PACK], BF16, name="woven", tag="woven", align_bytes=64)
+        for h in range(2):
+            nc.vector.tensor_copy(
+                out=woven[:, h * HALF * PACK : (h + 1) * HALF * PACK].rearrange("p (c i t) -> p c t i", i=4, t=PACK),
+                in_=xb_raw[h][:].rearrange("p t (c i) -> p c t i", i=4),
+            )
+        for h in range(2):
+            cols = slice(h * HALF, (h + 1) * HALF)
+            nc.vector.quantize_mx(
+                out=xb_c[:, cols].bitcast(FP8X4),
+                scales=xb_s[:, cols],
+                in_=woven[:, h * HALF * PACK : (h + 1) * HALF * PACK],
+            )
+
+        for i in range(TILES):
+            acc = psum.tile([P, S], F32, name=f"acc_b{i}", tag=f"pb{i}")
+            nc.tensor.matmul_mx(
+                out=acc[:],
+                lhsT=wb_c[:, 2 * P * i : 2 * P * (i + 1)].bitcast(FP4X4),
+                lhsT_scale=wb_s[:, P * i : P * (i + 1)],
+                rhs=xb_c[:].bitcast(FP8X4),
+                rhs_scale=xb_s[:],
+                start=True,
+                stop=True,
+            )
+            nc.scalar.copy(out=zb[i][:, :S], in_=acc[:])
+
+        def add_transposed(bank, src, first, last):
+            chunks = src.shape[1] // P
+            for c in range(chunks):
+                cols = slice(c * P, (c + 1) * P)
+                nc.tensor.matmul(
+                    bank[:, cols],
+                    lhsT=src[:, cols],
+                    rhs=ident[:],
+                    is_transpose=True,
+                    start=first and c == 0,
+                    stop=last and c == chunks - 1,
+                )
+
+        PIECES = [(0, 0, 512), (1, 0, 512), (2, 0, 256), (2, 256, 256), (3, 0, 256), (3, 256, 256)]
+        SQ = "ssssss"
+        UE = "gggggg"
+        PATH = "ppppvv"
+        UTAG = {}
+        ATAG = {2: "zb1", 3: "mag1"}
+        BTAG = {2: "mag0", 3: "root0"}
+        a01 = keep.tile([P, 2 * J], F32, name="a01", tag="woven", align_bytes=64)
+        side_a = {}
+        state = {}
+
+        def pick(k):
+            i, lo, width = PIECES[k]
+            cols = slice(lo, lo + width)
+            if lo == 0:
+                if i < 2:
+                    a = a01[:, i * J : (i + 1) * J]
+                    mag_a = keep.tile([P, J], F32, name=f"mag_a{i}", tag=("wb_c", "xb_c")[i], align_bytes=64)
+                else:
+                    a = keep.tile([P, J], F32, name=f"a{i}", tag=ATAG[i])[:]
+                    mag_a = keep.tile([P, J], F32, name=f"mag_a{i}")
+                nc.vector.tensor_copy(out=a, in_=za[:, i, :].indirect(list_a[:]))
+                nc.scalar.activation(out=mag_a[:], in_=a, func=ACT.Abs)
+                side_a[i] = (a, mag_a, keep.tile([P, J], F32, name=f"b{i}", tag=BTAG.get(i, f"b{i}")))
+            a, mag_a, b_all = side_a[i]
+            on_pe = PATH[k] == "p"
+            if on_pe:
+                den = psum.tile([P, width], F32, name=f"den{k}", tag=f"pb{k}")
+                add_transposed(den, mag_a[:, cols], True, False)
+            b = b_all[:, cols]
+            nc.vector.tensor_copy(out=b, in_=zb[i][:].indirect(list_b[:, lo // 16 : (lo + width) // 16]))
+            mag = keep.tile([P, width], F32, name=f"mag{k}", tag=f"mag{k}")
+            nc.scalar.activation(out=mag[:], in_=b, func=ACT.Abs)
+            if on_pe:
+                add_transposed(den, mag[:], False, True)
+            else:
+                den = keep.tile([P, width], F32, name=f"sum{k}")
+                (nc.gpsimd if PATH[k] == "g" else nc.vector).tensor_tensor(out=den[:], in0=mag_a[:, cols], in1=mag[:], op=ALU.add)
+            u = keep.tile([P, width], F32, name=f"u{k}", tag=UTAG.get(k, f"u{k}"))
+            (nc.gpsimd if UE[k] == "g" else nc.vector).tensor_tensor(out=u[:], in0=a[:, cols], in1=b, op=ALU.mult)
+            state[k] = (den, u)
+
+        def invert(k):
+            i, lo, width = PIECES[k]
+            den, u = state[k]
+            root = keep.tile([P, width], F32, name=f"root{k}", tag=f"root{k}")
+            nc.scalar.activation(out=root[:], in_=den[:], func=ACT.Abs_reciprocal_sqrt, bias=1.0)
+            inv = root
+            if SQ[k] != "v":
+                inv = keep.tile([P, width], F32, name=f"inv{k}")
+            if SQ[k] == "s":
+                nc.scalar.activation(out=inv[:], in_=root[:], func=ACT.Square)
+            if SQ[k] == "g":
+                nc.gpsimd.tensor_tensor(out=inv[:], in0=root[:], in1=root[:], op=ALU.mult)
+            state[k] = (inv, u)
+
+        def finish(k):
+            i, lo, width = PIECES[k]
+            back, u = state[k]
+            if PATH[k] == "p":
+                inv = back
+                back = psum.tile([P, width], F32, name=f"back{k}", tag=f"pa{k}")
+                for c in range(width // P):
+                    part = slice(c * P, (c + 1) * P)
+                    nc.tensor.transpose(back[:, part], inv[:, part], ident[:])
+            y = keep.tile([P, width], F32, name=f"y{k}")
+            if SQ[k] == "v":
+                t = keep.tile([P, width], F32, name=f"t{k}")
+                nc.vector.tensor_tensor(out=t[:], in0=u[:], in1=back[:], op=ALU.mult)
+                u = t
+            nc.vector.tensor_tensor(out=y[:], in0=u[:], in1=back[:], op=ALU.mult)
+            nc.sync.dma_start(out=out[P * i : P * (i + 1), lo : lo + width], in_=y[:])
+
+        for step, k in [(0,0),(0,1),(1,0),(0,2),(1,1),(2,0),(0,3),(1,2),(2,1),(0,4),(1,3),(0,5),(2,2),(1,4),(2,3),(1,5),(2,4),(2,5)]:
+            (pick, invert, finish)[step](k)

@@ -20,18 +20,20 @@ ACT = mybir.ActivationFunctionType
 P = 128
 PACK = 4
 TILES = N // P
+LAST = TILES - 1
 SPARE = 192
 HALF = S // 2
+QUARTER = S // 4
+PER_COLUMN = 16
+
+PIECES = [(i, 0, J) for i in range(LAST)] + [(LAST, 0, J // 2), (LAST, J // 2, J // 2)]
+TWICE = 2
 
 
-def load_scales(queue, plane, scales):
+def load_scales(nc, plane, scales):
     rows = scales[0].bitcast(I32)
     for q in range(4):
-        four = rows[4 * q : 4 * q + 4, :]
-        queue.dma_start(
-            out=plane[32 * q : 32 * q + 32, :].bitcast(I32),
-            in_=four.unsqueeze(0).broadcast_to([8, 4, rows.shape[1]]),
-        )
+        nc.sync.dma_start(out=plane[32 * q : 32 * q + 4, :].bitcast(I32), in_=rows[4 * q : 4 * q + 4, :])
 
 
 def tile_list_cross_lookup_product_kernel(
@@ -48,20 +50,24 @@ def tile_list_cross_lookup_product_kernel(
         wa_s = keep.tile([P, N], U8, name="wa_s", align_bytes=64)
         wb_c = keep.tile([P, 2 * N], U8, name="wb_c", tag="wb_c", align_bytes=64)
         wb_s = keep.tile([P, N], U8, name="wb_s", align_bytes=64)
-        list_a = keep.tile([P, J // 16], U16, name="list_a")
-        list_b = keep.tile([P, J // 16], U16, name="list_b")
+        list_a = keep.tile([P, J // PER_COLUMN], U16, name="list_a")
+        list_b = keep.tile([P, J // PER_COLUMN], U16, name="list_b")
         xb_rows = xb.rearrange("(p j) w -> p j w", j=PACK)
-        xb_raw = [keep.tile([P, PACK, HALF], F32, name=f"xb_raw{h}", tag=f"xb_raw{h}") for h in range(2)]
+        xb_raw = [
+            keep.tile([P, PACK, HALF], F32, name=f"xb_raw{h}", tag=f"xb_raw{h}", align_bytes=64) for h in range(2)
+        ]
 
-        load_scales(nc.sync, xa_s, xa_scales)
-        nc.sync.dma_start(out=xb_raw[0][:], in_=xb_rows[:, :, :HALF])
+        for plane in (xa_s, wa_s, wb_s):
+            nc.gpsimd.memset(plane[:].bitcast(I32), 0)
         nc.sync.dma_start(out=xa_c[:].bitcast(I32), in_=xa_words[0].bitcast(I32))
+        load_scales(nc, xa_s, xa_scales)
+        nc.sync.dma_start(out=xb_raw[0][:], in_=xb_rows[:, :, :HALF])
         nc.sync.dma_start(out=wa_c[:].bitcast(I32), in_=wa_words[0].rearrange("p n t -> p (n t)").bitcast(I32))
-        load_scales(nc.sync, wa_s, wa_scales)
+        load_scales(nc, wa_s, wa_scales)
         nc.sync.dma_start(out=xb_raw[1][:], in_=xb_rows[:, :, HALF:])
         nc.sync.dma_start(list_a[:], offs)
         nc.sync.dma_start(out=wb_c[:].bitcast(I32), in_=wb_words[0].bitcast(I32))
-        load_scales(nc.sync, wb_s, wb_scales)
+        load_scales(nc, wb_s, wb_scales)
         nc.sync.dma_start(list_b[:], offs2)
 
         one = keep.tile([P, 1], F32, name="one")
@@ -78,7 +84,7 @@ def tile_list_cross_lookup_product_kernel(
         make_identity(nc, ident[:])
 
         for i in range(TILES):
-            acc = psum.tile([P, T], F32, name=f"acc_a{i}", tag=f"pa{i}")
+            acc = psum.tile([P, T], F32, name=f"acc_a{i}", tag=f"bank_a{i}")
             nc.tensor.matmul_mx(
                 out=acc[:],
                 lhsT=wa_c[:, 4 * P * i : 4 * P * (i + 1)].bitcast(FP8X4),
@@ -93,21 +99,24 @@ def tile_list_cross_lookup_product_kernel(
         xb_c = keep.tile([P, S], U32, name="xb_c", tag="xb_c", align_bytes=64)
         xb_s = keep.tile([P, S], U8, name="xb_s", align_bytes=64)
         woven = keep.tile([P, S * PACK], BF16, name="woven", tag="woven", align_bytes=64)
-        for h in range(2):
+        for g in range(S // QUARTER):
+            h, lo = divmod(g * QUARTER, HALF)
             nc.vector.tensor_copy(
-                out=woven[:, h * HALF * PACK : (h + 1) * HALF * PACK].rearrange("p (c i t) -> p c t i", i=4, t=PACK),
-                in_=xb_raw[h][:].rearrange("p t (c i) -> p c t i", i=4),
+                out=woven[:, g * QUARTER * PACK : (g + 1) * QUARTER * PACK].rearrange(
+                    "p (c i t) -> p c t i", i=4, t=PACK
+                ),
+                in_=xb_raw[h][:, :, lo : lo + QUARTER].rearrange("p t (c i) -> p c t i", i=4),
             )
-        for h in range(2):
-            cols = slice(h * HALF, (h + 1) * HALF)
+        for g in range(S // QUARTER):
+            cols = slice(g * QUARTER, (g + 1) * QUARTER)
             nc.vector.quantize_mx(
                 out=xb_c[:, cols].bitcast(FP8X4),
                 scales=xb_s[:, cols],
-                in_=woven[:, h * HALF * PACK : (h + 1) * HALF * PACK],
+                in_=woven[:, g * QUARTER * PACK : (g + 1) * QUARTER * PACK],
             )
 
         for i in range(TILES):
-            acc = psum.tile([P, S], F32, name=f"acc_b{i}", tag=f"pb{i}")
+            acc = psum.tile([P, S], F32, name=f"acc_b{i}", tag=f"bank_b{i}")
             nc.tensor.matmul_mx(
                 out=acc[:],
                 lhsT=wb_c[:, 2 * P * i : 2 * P * (i + 1)].bitcast(FP4X4),
@@ -119,7 +128,12 @@ def tile_list_cross_lookup_product_kernel(
             )
             nc.scalar.copy(out=zb[i][:, :S], in_=acc[:])
 
-        def add_transposed(bank, src, first, last):
+        a_home = [("xb_raw1", 64), ("woven", 64), ("zb1", None), ("mag_b0", None)]
+        mag_a_home = [("wb_c", 64), ("xb_c", 64), ("mag_a2", None), ("mag_a3", None)]
+        b_home = ["b0", "b1", "b2", "mag_b1"]
+        a, b, mag_a, den, factor, product = {}, {}, {}, {}, {}, {}
+
+        def add_transposed(bank, src, first):
             chunks = src.shape[1] // P
             for c in range(chunks):
                 cols = slice(c * P, (c + 1) * P)
@@ -129,81 +143,69 @@ def tile_list_cross_lookup_product_kernel(
                     rhs=ident[:],
                     is_transpose=True,
                     start=first and c == 0,
-                    stop=last and c == chunks - 1,
+                    stop=not first and c == chunks - 1,
                 )
-
-        PIECES = [(0, 0, 512), (1, 0, 512), (2, 0, 256), (2, 256, 256), (3, 0, 256), (3, 256, 256)]
-        SQ = "ssssss"
-        UE = "gggggg"
-        PATH = "ppppvv"
-        UTAG = {}
-        ATAG = {2: "zb1", 3: "mag1"}
-        BTAG = {2: "mag0", 3: "root0"}
-        a01 = keep.tile([P, 2 * J], F32, name="a01", tag="woven", align_bytes=64)
-        side_a = {}
-        state = {}
 
         def pick(k):
             i, lo, width = PIECES[k]
             cols = slice(lo, lo + width)
             if lo == 0:
-                if i < 2:
-                    a = a01[:, i * J : (i + 1) * J]
-                    mag_a = keep.tile([P, J], F32, name=f"mag_a{i}", tag=("wb_c", "xb_c")[i], align_bytes=64)
-                else:
-                    a = keep.tile([P, J], F32, name=f"a{i}", tag=ATAG[i])[:]
-                    mag_a = keep.tile([P, J], F32, name=f"mag_a{i}")
-                nc.vector.tensor_copy(out=a, in_=za[:, i, :].indirect(list_a[:]))
-                nc.scalar.activation(out=mag_a[:], in_=a, func=ACT.Abs)
-                side_a[i] = (a, mag_a, keep.tile([P, J], F32, name=f"b{i}", tag=BTAG.get(i, f"b{i}")))
-            a, mag_a, b_all = side_a[i]
-            on_pe = PATH[k] == "p"
-            if on_pe:
-                den = psum.tile([P, width], F32, name=f"den{k}", tag=f"pb{k}")
-                add_transposed(den, mag_a[:, cols], True, False)
-            b = b_all[:, cols]
-            nc.vector.tensor_copy(out=b, in_=zb[i][:].indirect(list_b[:, lo // 16 : (lo + width) // 16]))
-            mag = keep.tile([P, width], F32, name=f"mag{k}", tag=f"mag{k}")
-            nc.scalar.activation(out=mag[:], in_=b, func=ACT.Abs)
-            if on_pe:
-                add_transposed(den, mag[:], False, True)
-            else:
-                den = keep.tile([P, width], F32, name=f"sum{k}")
-                (nc.gpsimd if PATH[k] == "g" else nc.vector).tensor_tensor(out=den[:], in0=mag_a[:, cols], in1=mag[:], op=ALU.add)
-            u = keep.tile([P, width], F32, name=f"u{k}", tag=UTAG.get(k, f"u{k}"))
-            (nc.gpsimd if UE[k] == "g" else nc.vector).tensor_tensor(out=u[:], in0=a[:, cols], in1=b, op=ALU.mult)
-            state[k] = (den, u)
+                a[i] = keep.tile([P, J], F32, name=f"a{i}", tag=a_home[i][0], align_bytes=a_home[i][1])
+                mag_a[i] = keep.tile(
+                    [P, J], F32, name=f"mag_a{i}", tag=mag_a_home[i][0], align_bytes=mag_a_home[i][1]
+                )
+                nc.vector.tensor_copy(out=a[i][:], in_=za[:, i, :].indirect(list_a[:]))
+                nc.scalar.activation(out=mag_a[i][:], in_=a[i][:], func=ACT.Abs)
+                b[i] = keep.tile([P, J], F32, name=f"b{i}", tag=b_home[i])
+            den[k] = psum.tile([P, width], F32, name=f"den{k}", tag=f"bank_b{k % TILES}")
+            add_transposed(den[k], mag_a[i][:, cols], True)
+            entries = list_b[:, lo // PER_COLUMN : (lo + width) // PER_COLUMN]
+            nc.vector.tensor_copy(out=b[i][:, cols], in_=zb[i][:].indirect(entries))
+            mag_b = keep.tile([P, width], F32, name=f"mag_b{k}", tag=f"mag_b{k}")
+            nc.scalar.activation(out=mag_b[:], in_=b[i][:, cols], func=ACT.Abs)
+            add_transposed(den[k], mag_b[:], False)
+            if i < LAST:
+                product[i] = keep.tile([P, J], F32, name=f"product{i}", tag=f"product{i}")
+                nc.gpsimd.tensor_tensor(out=product[i][:], in0=a[i][:], in1=b[i][:], op=ALU.mult)
 
         def invert(k):
-            i, lo, width = PIECES[k]
-            den, u = state[k]
-            root = keep.tile([P, width], F32, name=f"root{k}", tag=f"root{k}")
-            nc.scalar.activation(out=root[:], in_=den[:], func=ACT.Abs_reciprocal_sqrt, bias=1.0)
-            inv = root
-            if SQ[k] != "v":
-                inv = keep.tile([P, width], F32, name=f"inv{k}")
-            if SQ[k] == "s":
-                nc.scalar.activation(out=inv[:], in_=root[:], func=ACT.Square)
-            if SQ[k] == "g":
-                nc.gpsimd.tensor_tensor(out=inv[:], in0=root[:], in1=root[:], op=ALU.mult)
-            state[k] = (inv, u)
+            width = PIECES[k][2]
+            factor[k] = keep.tile([P, width], F32, name=f"root{k}")
+            nc.scalar.activation(out=factor[k][:], in_=den[k][:], func=ACT.Abs_reciprocal_sqrt, bias=1.0)
+            if k >= TWICE:
+                root = factor[k]
+                factor[k] = keep.tile([P, width], F32, name=f"inverse{k}")
+                nc.scalar.activation(out=factor[k][:], in_=root[:], func=ACT.Square)
 
-        def finish(k):
+        def finish(k, once):
             i, lo, width = PIECES[k]
-            back, u = state[k]
-            if PATH[k] == "p":
-                inv = back
-                back = psum.tile([P, width], F32, name=f"back{k}", tag=f"pa{k}")
-                for c in range(width // P):
-                    part = slice(c * P, (c + 1) * P)
-                    nc.tensor.transpose(back[:, part], inv[:, part], ident[:])
+            u = product[i][:, lo : lo + width]
+            bank = f"bank_a{k}" if k < TILES else "bank_b1"
+            back = psum.tile([P, width], F32, name=f"back{k}", tag=bank)
+            for c in range(width // P):
+                cols = slice(c * P, (c + 1) * P)
+                nc.tensor.transpose(back[:, cols], factor[k][:, cols], ident[:])
             y = keep.tile([P, width], F32, name=f"y{k}")
-            if SQ[k] == "v":
-                t = keep.tile([P, width], F32, name=f"t{k}")
-                nc.vector.tensor_tensor(out=t[:], in0=u[:], in1=back[:], op=ALU.mult)
-                u = t
-            nc.vector.tensor_tensor(out=y[:], in0=u[:], in1=back[:], op=ALU.mult)
+            if k < TWICE:
+                halves = (slice(0, width // 2), slice(width // 2, width))
+                for cols in halves:
+                    nc.vector.tensor_tensor(out=once[:, cols], in0=u[:, cols], in1=back[:, cols], op=ALU.mult)
+                for cols in halves:
+                    nc.vector.tensor_tensor(out=y[:, cols], in0=once[:, cols], in1=back[:, cols], op=ALU.mult)
+            else:
+                nc.vector.tensor_tensor(out=y[:], in0=u, in1=back[:], op=ALU.mult)
             nc.sync.dma_start(out=out[P * i : P * (i + 1), lo : lo + width], in_=y[:])
 
-        for step, k in [(0,0),(0,1),(1,0),(0,2),(1,1),(2,0),(0,3),(1,2),(2,1),(0,4),(1,3),(0,5),(2,2),(1,4),(2,3),(1,5),(2,4),(2,5)]:
-            (pick, invert, finish)[step](k)
+        for k in range(len(PIECES) + 1):
+            if k < len(PIECES):
+                pick(k)
+            if k > 0:
+                invert(k - 1)
+
+        once = keep.tile([P, TWICE, J], F32, name="once", tag="mag_b2")
+        for k in range(TWICE):
+            finish(k, once[:, k, :])
+        product[LAST] = keep.tile([P, J], F32, name=f"product{LAST}", tag="product0")
+        nc.vector.tensor_tensor(out=product[LAST][:], in0=a[LAST][:], in1=b[LAST][:], op=ALU.mult)
+        for k in range(TWICE, len(PIECES)):
+            finish(k, None)

from contextlib import ExitStack

import concourse.mybir as mybir
from concourse.masks import make_identity

K = L = T = S = J = N = 512
FLOPS = 2 * K * N * T + 2 * L * N * S

F32 = mybir.dt.float32
BF16 = mybir.dt.bfloat16
I32 = mybir.dt.int32
U32 = mybir.dt.uint32
U16 = mybir.dt.uint16
U8 = mybir.dt.uint8
FP8X4 = mybir.dt.float8_e4m3fn_x4
FP4X4 = mybir.dt.float4_e2m1fn_x4
ALU = mybir.AluOpType
ACT = mybir.ActivationFunctionType

P = 128
PACK = 4
TILES = N // P
LAST = TILES - 1
SPARE = 192
HALF = S // 2
QUARTER = S // 4
PER_COLUMN = 16

PIECES = [(i, 0, J) for i in range(LAST)] + [(LAST, 0, J // 2), (LAST, J // 2, J // 2)]
TWICE = 2


def load_scales(nc, plane, scales):
    rows = scales[0].bitcast(I32)
    for q in range(4):
        nc.sync.dma_start(out=plane[32 * q : 32 * q + 4, :].bitcast(I32), in_=rows[4 * q : 4 * q + 4, :])


def tile_list_cross_lookup_product_kernel(
    tc, xa_words, xa_scales, wa_words, wa_scales, xb, wb_words, wb_scales, offs, offs2, out
):
    nc = tc.nc
    with ExitStack() as ctx:
        keep = ctx.enter_context(tc.tile_pool(name="keep", bufs=1))
        psum = ctx.enter_context(tc.psum_pool(name="psum", bufs=1))

        xa_c = keep.tile([P, 2 * T], U8, name="xa_c", align_bytes=64)
        xa_s = keep.tile([P, T], U8, name="xa_s", align_bytes=64)
        wa_c = keep.tile([P, 4 * N], U8, name="wa_c", align_bytes=64)
        wa_s = keep.tile([P, N], U8, name="wa_s", align_bytes=64)
        wb_c = keep.tile([P, 2 * N], U8, name="wb_c", tag="wb_c", align_bytes=64)
        wb_s = keep.tile([P, N], U8, name="wb_s", align_bytes=64)
        list_a = keep.tile([P, J // PER_COLUMN], U16, name="list_a")
        list_b = keep.tile([P, J // PER_COLUMN], U16, name="list_b")
        xb_rows = xb.rearrange("(p j) w -> p j w", j=PACK)
        xb_raw = [
            keep.tile([P, PACK, HALF], F32, name=f"xb_raw{h}", tag=f"xb_raw{h}", align_bytes=64) for h in range(2)
        ]

        for plane in (xa_s, wa_s, wb_s):
            nc.gpsimd.memset(plane[:].bitcast(I32), 0)
        nc.sync.dma_start(out=xa_c[:].bitcast(I32), in_=xa_words[0].bitcast(I32))
        load_scales(nc, xa_s, xa_scales)
        nc.sync.dma_start(out=xb_raw[0][:], in_=xb_rows[:, :, :HALF])
        nc.sync.dma_start(out=wa_c[:].bitcast(I32), in_=wa_words[0].rearrange("p n t -> p (n t)").bitcast(I32))
        load_scales(nc, wa_s, wa_scales)
        nc.sync.dma_start(out=xb_raw[1][:], in_=xb_rows[:, :, HALF:])
        nc.sync.dma_start(list_a[:], offs)
        nc.sync.dma_start(out=wb_c[:].bitcast(I32), in_=wb_words[0].bitcast(I32))
        load_scales(nc, wb_s, wb_scales)
        nc.sync.dma_start(list_b[:], offs2)

        one = keep.tile([P, 1], F32, name="one")
        warm = keep.tile([P, 1], F32, name="warm")
        nc.vector.memset(one[:], 1.0)
        nc.scalar.activation(out=warm[:], in_=one[:], func=ACT.Abs_reciprocal_sqrt)

        za = keep.tile([P, TILES, T + SPARE], F32, name="za")
        zb = [keep.tile([P, S + SPARE], F32, name=f"zb{i}", tag=f"zb{i}") for i in range(TILES)]
        nc.vector.memset(za[:, :, T:], 0.0)
        for i in range(TILES):
            nc.gpsimd.memset(zb[i][:, S:], 0.0)
        ident = keep.tile([P, P], F32, name="ident")
        make_identity(nc, ident[:])

        for i in range(TILES):
            acc = psum.tile([P, T], F32, name=f"acc_a{i}", tag=f"bank_a{i}")
            nc.tensor.matmul_mx(
                out=acc[:],
                lhsT=wa_c[:, 4 * P * i : 4 * P * (i + 1)].bitcast(FP8X4),
                lhsT_scale=wa_s[:, P * i : P * (i + 1)],
                rhs=xa_c[:].bitcast(FP4X4),
                rhs_scale=xa_s[:],
                start=True,
                stop=True,
            )
            nc.scalar.copy(out=za[:, i, :T], in_=acc[:])

        xb_c = keep.tile([P, S], U32, name="xb_c", tag="xb_c", align_bytes=64)
        xb_s = keep.tile([P, S], U8, name="xb_s", align_bytes=64)
        woven = keep.tile([P, S * PACK], BF16, name="woven", tag="woven", align_bytes=64)
        for g in range(S // QUARTER):
            h, lo = divmod(g * QUARTER, HALF)
            nc.vector.tensor_copy(
                out=woven[:, g * QUARTER * PACK : (g + 1) * QUARTER * PACK].rearrange(
                    "p (c i t) -> p c t i", i=4, t=PACK
                ),
                in_=xb_raw[h][:, :, lo : lo + QUARTER].rearrange("p t (c i) -> p c t i", i=4),
            )
        for g in range(S // QUARTER):
            cols = slice(g * QUARTER, (g + 1) * QUARTER)
            nc.vector.quantize_mx(
                out=xb_c[:, cols].bitcast(FP8X4),
                scales=xb_s[:, cols],
                in_=woven[:, g * QUARTER * PACK : (g + 1) * QUARTER * PACK],
            )

        for i in range(TILES):
            acc = psum.tile([P, S], F32, name=f"acc_b{i}", tag=f"bank_b{i}")
            nc.tensor.matmul_mx(
                out=acc[:],
                lhsT=wb_c[:, 2 * P * i : 2 * P * (i + 1)].bitcast(FP4X4),
                lhsT_scale=wb_s[:, P * i : P * (i + 1)],
                rhs=xb_c[:].bitcast(FP8X4),
                rhs_scale=xb_s[:],
                start=True,
                stop=True,
            )
            nc.scalar.copy(out=zb[i][:, :S], in_=acc[:])

        a_home = [("xb_raw1", 64), ("woven", 64), ("zb1", None), ("mag_b0", None)]
        mag_a_home = [("wb_c", 64), ("xb_c", 64), ("mag_a2", None), ("mag_a3", None)]
        b_home = ["b0", "b1", "b2", "mag_b1"]
        a, b, mag_a, den, factor, product = {}, {}, {}, {}, {}, {}

        def add_transposed(bank, src, first):
            chunks = src.shape[1] // P
            for c in range(chunks):
                cols = slice(c * P, (c + 1) * P)
                nc.tensor.matmul(
                    bank[:, cols],
                    lhsT=src[:, cols],
                    rhs=ident[:],
                    is_transpose=True,
                    start=first and c == 0,
                    stop=not first and c == chunks - 1,
                )

        def pick(k):
            i, lo, width = PIECES[k]
            cols = slice(lo, lo + width)
            if lo == 0:
                a[i] = keep.tile([P, J], F32, name=f"a{i}", tag=a_home[i][0], align_bytes=a_home[i][1])
                mag_a[i] = keep.tile(
                    [P, J], F32, name=f"mag_a{i}", tag=mag_a_home[i][0], align_bytes=mag_a_home[i][1]
                )
                nc.vector.tensor_copy(out=a[i][:], in_=za[:, i, :].indirect(list_a[:]))
                nc.scalar.activation(out=mag_a[i][:], in_=a[i][:], func=ACT.Abs)
                b[i] = keep.tile([P, J], F32, name=f"b{i}", tag=b_home[i])
            den[k] = psum.tile([P, width], F32, name=f"den{k}", tag=f"bank_b{k % TILES}")
            add_transposed(den[k], mag_a[i][:, cols], True)
            entries = list_b[:, lo // PER_COLUMN : (lo + width) // PER_COLUMN]
            nc.vector.tensor_copy(out=b[i][:, cols], in_=zb[i][:].indirect(entries))
            mag_b = keep.tile([P, width], F32, name=f"mag_b{k}", tag=f"mag_b{k}")
            nc.scalar.activation(out=mag_b[:], in_=b[i][:, cols], func=ACT.Abs)
            add_transposed(den[k], mag_b[:], False)
            if i < LAST:
                product[i] = keep.tile([P, J], F32, name=f"product{i}", tag=f"product{i}")
                nc.gpsimd.tensor_tensor(out=product[i][:], in0=a[i][:], in1=b[i][:], op=ALU.mult)

        def invert(k):
            width = PIECES[k][2]
            factor[k] = keep.tile([P, width], F32, name=f"root{k}")
            nc.scalar.activation(out=factor[k][:], in_=den[k][:], func=ACT.Abs_reciprocal_sqrt, bias=1.0)
            if k >= TWICE:
                root = factor[k]
                factor[k] = keep.tile([P, width], F32, name=f"inverse{k}")
                nc.scalar.activation(out=factor[k][:], in_=root[:], func=ACT.Square)

        def finish(k, once):
            i, lo, width = PIECES[k]
            u = product[i][:, lo : lo + width]
            bank = f"bank_a{k}" if k < TILES else "bank_b1"
            back = psum.tile([P, width], F32, name=f"back{k}", tag=bank)
            for c in range(width // P):
                cols = slice(c * P, (c + 1) * P)
                nc.tensor.transpose(back[:, cols], factor[k][:, cols], ident[:])
            y = keep.tile([P, width], F32, name=f"y{k}")
            if k < TWICE:
                halves = (slice(0, width // 2), slice(width // 2, width))
                for cols in halves:
                    nc.vector.tensor_tensor(out=once[:, cols], in0=u[:, cols], in1=back[:, cols], op=ALU.mult)
                for cols in halves:
                    nc.vector.tensor_tensor(out=y[:, cols], in0=once[:, cols], in1=back[:, cols], op=ALU.mult)
            else:
                nc.vector.tensor_tensor(out=y[:], in0=u, in1=back[:], op=ALU.mult)
            nc.sync.dma_start(out=out[P * i : P * (i + 1), lo : lo + width], in_=y[:])

        for k in range(len(PIECES) + 1):
            if k < len(PIECES):
                pick(k)
            if k > 0:
                invert(k - 1)

        once = keep.tile([P, TWICE, J], F32, name="once", tag="mag_b2")
        for k in range(TWICE):
            finish(k, once[:, k, :])
        product[LAST] = keep.tile([P, J], F32, name=f"product{LAST}", tag="product0")
        nc.vector.tensor_tensor(out=product[LAST][:], in0=a[LAST][:], in1=b[LAST][:], op=ALU.mult)
        for k in range(TWICE, len(PIECES)):
            finish(k, None)
